import numpy as np, ml_dtypes
CORES = [25,29,65,69,153,157,193,197]
N = 8
import mx_ref
NC = 256
CNT = [[0,0,24,24,0,8,200,0],[8,0,0,0,24,96,104,24],[0,80,48,0,72,40,0,16],[32,0,8,0,64,0,32,120],[96,8,0,88,0,0,64,0],[24,0,64,64,0,0,64,40],[48,64,72,0,32,0,0,40],[32,64,72,0,40,0,0,48]]
OFF = [[sum(c[:e]) for e in range(N + 1)] for c in CNT]
TOT = [sum(c[e] for c in CNT) for e in range(N)]
BF = ml_dtypes.bfloat16
def setup_inputs(rng):
    def f(*shape):
        return mx_ref.flush((rng.standard_normal(shape, dtype=np.float32) * np.exp2(rng.integers(-2, 3, shape[:-1] + (1,)))).astype(BF))
    return {"w": f(N, 128, 512), "x": f(N, 128, 4 * NC)}
def setup_inputs_blocks(rng):
    d = setup_inputs(rng)
    for k in ("w", "x"): d[k] = mx_ref.spread(d[k], rng, 4)
    return d
def setup_inputs_wide(rng):
    d = setup_inputs(rng)
    for k in ("w", "x"): d[k] = mx_ref.flush((d[k].astype(np.float32) * np.exp2(rng.integers(-10, 11, (N, 1, 1))).astype(np.float32)).astype(BF))
    return d
def setup_inputs_zeros(rng):
    d = setup_inputs(rng); v = d["x"].reshape(N, 128, -1, 4).copy()
    v[np.broadcast_to((rng.random((N, 1, v.shape[2], 1)) < 0.33), v.shape)] = 0
    d["x"] = v.reshape(d["x"].shape)
    return d
def reference(w, x):
    y = np.full((N, 128, max(TOT)), np.nan, np.float32)
    for e in range(N):
        t = np.concatenate([x[j][:, 4 * OFF[j][e]:4 * OFF[j][e + 1]] for j in range(N)], axis=1)
        y[e][:, :TOT[e]] = mx_ref.matmul(mx_ref.quantize(w[e]), mx_ref.quantize(t))
    return {"y": y}

@@ -1,0 +1,207 @@
+from concourse.bass import DstId, RemoteDMATransfer
+from concourse.mybir import dt, ActivationFunctionType
+
+MINCOLS = 128
+BANK = 512
+
+SCRATCH = {
+    "xb": ("sbuf", [128, 1024], "bfloat16"),
+    "wb": ("sbuf", [128, 512], "bfloat16"),
+    "xq": ("sbuf", [128, 256], "float8_e4m3fn_x4"),
+    "xs": ("sbuf", [128, 256], "uint8"),
+    "wq": ("sbuf", [128, 128], "float8_e4m3fn_x4"),
+    "ws": ("sbuf", [128, 128], "uint8"),
+    "bq": ("sbuf", [128, 464], "float8_e4m3fn_x4"),
+    "bs": ("sbuf", [128, 464], "uint8"),
+    "ysb": ("sbuf", [128, 464], "float32"),
+    "ps": ("psum", [128, 3 * BANK], "float32"),
+}
+SEMAPHORES = ["ldx", "ldw", "qx", "qw", "hop", "arr0", "arr1", "sent", "mmo", "mm0", "mm1", "cp0", "cp1", "st0", "st1"]
+
+_MEMO = {}
+
+
+def _bits(mask):
+    return [b for b in range(mask.bit_length()) if (mask >> b) & 1]
+
+
+def _pick(mask, start, n):
+    m = 0
+    for b in _bits(mask)[start:start + n]:
+        m |= 1 << b
+    return m
+
+
+def _pair_up(items, first_alone):
+    calls, rest = [], list(items)
+    while rest:
+        a = rest.pop(0)
+        mate = None
+        if not (first_alone and not calls):
+            for b in rest:
+                if b["bytes"] == a["bytes"]:
+                    mate = b
+                    break
+        if mate is None:
+            calls.append([a])
+        else:
+            rest.remove(mate)
+            calls.append([a, mate])
+    return calls
+
+
+def _plan(T, topo):
+    cores, cnt = list(T.cores), T.tables["CNT"]
+    n = len(cores)
+    off = [[sum(r[:e]) for e in range(n + 1)] for r in cnt]
+    tot = [sum(cnt[j][e] for j in range(n)) for e in range(n)]
+    land = [[sum(cnt[i][e] for i in range(j) if i != e) for j in range(n + 1)] for e in range(n)]
+
+    cut = []
+    for e in range(n):
+        edges = [b for b in land[e] if b >= MINCOLS and land[e][n] - b >= MINCOLS]
+        cut.append(min(edges, key=lambda b: abs(2 * b - land[e][n])) if edges else None)
+
+    def run(kind, j, e):
+        piece = 1 if cut[e] is not None and land[e][j] >= cut[e] else 0
+        return {"kind": kind, "dst": cores[e], "buf": "b", "src_lo": off[j][e], "dst_lo": land[e][j], "w": cnt[j][e],
+                "bytes": cnt[j][e] * (1 if kind else 4), "sem": "arr%d" % piece}
+
+    def same_chip(a, b):
+        return topo.host(a) == topo.host(b) and topo.chip(a) == topo.chip(b)
+
+    calls = {}
+    for j, c in enumerate(cores):
+        todo = sorted([e for e in range(n) if e != j and cnt[j][e]], key=lambda e: -tot[e])
+        far = [e for e in todo if not topo.may_write(c, cores[e])]
+        near = [e for e in todo if topo.may_write(c, cores[e])]
+        mine = []
+        if far:
+            chipmates = [k for k in range(max(0, c - topo.CORES_PER_CHIP), c + topo.CORES_PER_CHIP)
+                         if same_chip(k, c) and k not in cores]
+            helpers = [k for k in chipmates if topo.die(k) == topo.die(c) and all(topo.may_write(k, d) for d in cores)]
+            lo, hi = min(off[j][e] for e in far), max(off[j][e + 1] for e in far)
+            for kind in (0, 1):
+                mine.append([{"kind": kind, "dst": helpers[kind], "buf": "x", "src_lo": lo, "dst_lo": lo, "w": hi - lo,
+                              "bytes": (hi - lo) * (1 if kind else 4), "sem": "hop"}])
+                calls[helpers[kind]] = _pair_up([run(kind, j, e) for e in far], True)
+        calls[c] = mine + _pair_up([run(kind, j, e) for e in near for kind in (0, 1)], False)
+
+    need, sent = {}, {}
+    for c, cl in calls.items():
+        leaving = 0
+        for call in cl:
+            for t in call:
+                if not same_chip(c, t["dst"]):
+                    leaving |= topo.mask(c, t["dst"])
+        for call in cl:
+            for t in call:
+                m = topo.mask(c, t["dst"])
+                t["mask"] = (m & ~leaving) or m if same_chip(c, t["dst"]) else m
+            if len(call) > 1 and call[0]["mask"] & call[1]["mask"]:
+                half = min(len(_bits(t["mask"])) for t in call) // 2
+                for i, t in enumerate(call):
+                    t["mask"] = _pick(t["mask"], i * half, half)
+            for t in call:
+                k = len(_bits(t["mask"]))
+                need[(t["dst"], t["sem"])] = need.get((t["dst"], t["sem"]), 0) + k
+                sent[c] = sent.get(c, 0) + k
+    return {"off": off, "tot": tot, "land": land, "cut": cut, "calls": calls, "need": need, "sent": sent, "cnt": cnt}
+
+
+def _issue(g, T, topo, core, call):
+    trs = []
+    for t in call:
+        a, b, w = t["src_lo"], t["dst_lo"], t["w"]
+        if t["kind"] == 0:
+            src = T.xq[:, a:a + w].bitcast(dt.uint8)
+            dst = (T.xq if t["buf"] == "x" else T.bq)[:, b:b + w].bitcast(dt.uint8)
+        else:
+            src = T.xs[:, a:a + w]
+            dst = (T.xs if t["buf"] == "x" else T.bs)[:, b:b + w]
+        rid, pid = topo.addr(t["dst"], core)
+        trs.append((dst, src, T.sem[t["sem"]], pid, rid, t["mask"]))
+    if len(trs) == 1:
+        dst, src, sem, pid, rid, mask = trs[0]
+        g.remote_dma(out_ap=dst, in_ap=src, remote_sem=sem, local_sem=T.sem.sent, pid=pid, routing_id=rid,
+                     dma_engine_mask=mask)
+    else:
+        g.remote_dma_fused([RemoteDMATransfer(dst_ids=[DstId(rid=rid, pnc=pid)], dma_engine_mask=mask, remote_sem=sem,
+                                              src=src, dst=dst) for dst, src, sem, pid, rid, mask in trs],
+                           local_sem=T.sem.sent)
+
+
+def rank_program(g, core, T, topo):
+    if "plan" not in _MEMO:
+        _MEMO["plan"] = _plan(T, topo)
+    P = _MEMO["plan"]
+    S = T.sem
+    rank = T.rank_of(core)
+    calls = P["calls"].get(core, [])
+
+    if rank is None:
+        if not calls:
+            return
+        g.wait_ge(S.hop, P["need"][(core, "hop")])
+        for call in calls:
+            _issue(g, T, topo, core, call)
+        g.wait_ge(S.sent, P["sent"][core])
+        return
+
+    e, cnt, off, land, n = rank, P["cnt"], P["off"], P["land"], len(P["cnt"])
+    own = cnt[e][e]
+    ncols = T.xq.shape[1]
+
+    g.sync.dma_start(T.xb[:], T.x[:]).then_inc(S.ldx, 16)
+    g.sync.dma_start(T.wb[:], T.w[:]).then_inc(S.ldw, 16)
+    g.vector.wait_ge(S.ldx, 16)
+    g.vector.quantize_mx(T.xq[:], T.xs[:], T.xb[:]).then_inc(S.qx, 1)
+    g.vector.wait_ge(S.ldw, 16)
+    g.vector.quantize_mx(T.wq[:], T.ws[:], T.wb[:]).then_inc(S.qw, 1)
+
+    g.wait_ge(S.qx, 1)
+    for call in calls:
+        _issue(g, T, topo, core, call)
+
+    total, c = land[e][n], P["cut"][e]
+    pieces = [(0, total, 0)] if c is None else [(0, c, 0), (c, total, 1)]
+
+    def widest(p):
+        return max(cnt[j][e] for j in range(n) if j != e and p[0] <= land[e][j] < p[1])
+    pieces.sort(key=widest)
+    own_at = land[e][e]
+
+    g.tensor.wait_ge(S.qw, 1)
+    if own:
+        a = min(off[e][e], ncols - MINCOLS)
+        g.tensor.wait_ge(S.qx, 1)
+        g.tensor.matmul_mx(T.ps[:, 2 * BANK:2 * BANK + MINCOLS], T.wq[:], T.ws[:], T.xq[:, a:a + MINCOLS],
+                           T.xs[:, a:a + MINCOLS], True, True).then_inc(S.mmo, 1)
+        home = [k for k, p in enumerate(pieces) if p[0] <= own_at <= p[1]][0]
+        g.vector.wait_ge(S.mmo, 1)
+        g.vector.tensor_copy(T.ysb[:, own_at:own_at + own],
+                             T.ps[:, 2 * BANK + off[e][e] - a:2 * BANK + off[e][e] - a + own]).then_inc(S["cp%d" % home], 1)
+
+    for k, (lo, hi, piece) in enumerate(pieces):
+        g.tensor.wait_ge(S["arr%d" % piece], P["need"][(core, "arr%d" % piece)])
+        g.tensor.matmul_mx(T.ps[:, k * BANK:k * BANK + hi - lo], T.wq[:], T.ws[:], T.bq[:, lo:hi], T.bs[:, lo:hi],
+                           True, True).then_inc(S["mm%d" % k], 1)
+        segs = [(lo, hi, 0)] if not own else [s for s in ((lo, min(hi, own_at), 0), (max(lo, own_at), hi, own)) if s[0] < s[1]]
+        eng, queue = (g.vector, g.sync) if k == 0 else (g.scalar, g.scalar)
+        eng.wait_ge(S["mm%d" % k], 1)
+        done = 0
+        for a, b, shift in segs:
+            src, dst = T.ps[:, k * BANK + a - lo:k * BANK + b - lo], T.ysb[:, a + shift:b + shift]
+            if k == 0:
+                eng.tensor_copy(dst, src).then_inc(S["cp%d" % k], 1)
+            else:
+                eng.activation(dst, src, ActivationFunctionType.Copy).then_inc(S["cp%d" % k], 1)
+            done += 1
+        y0, y1 = min(s[0] + s[2] for s in segs), max(s[1] + s[2] for s in segs)
+        if own and home == k:
+            y0, y1, done = min(y0, own_at), max(y1, own_at + own), done + 1
+        queue.wait_ge(S["cp%d" % k], done)
+        queue.dma_start(T.y[:, y0:y1], T.ysb[:, y0:y1]).then_inc(S["st%d" % k], 16)
+        queue.wait_ge(S["st%d" % k], 16)
+
+    g.wait_ge(S.sent, P["sent"][core])

@@ -14,9 +14,10 @@ SCRATCH = {
     "bq": ("sbuf", [128, 464], "float8_e4m3fn_x4"),
     "bs": ("sbuf", [128, 464], "uint8"),
     "ysb": ("sbuf", [128, 464], "float32"),
-    "ps": ("psum", [128, 3 * BANK], "float32"),
+    "ps": ("psum", [128, 5 * BANK], "float32"),
 }
-SEMAPHORES = ["ldx", "ldw", "qx", "qw", "hop", "arr0", "arr1", "sent", "mmo", "mm0", "mm1", "cp0", "cp1", "st0", "st1"]
+SEMAPHORES = ["ld0", "ld1", "ldw", "q0", "q1", "qw", "hop0", "hop1", "arr0", "arr1", "arr2", "arr3", "sent", "mmo", "mm0",
+              "mm1", "mm2", "mm3", "cpo", "cp0", "cp1", "cp2", "cp3", "sts", "stc"]
 
 _MEMO = {}
 
@@ -55,37 +56,135 @@ def _plan(T, topo):
     n = len(cores)
     off = [[sum(r[:e]) for e in range(n + 1)] for r in cnt]
     tot = [sum(cnt[j][e] for j in range(n)) for e in range(n)]
-    land = [[sum(cnt[i][e] for i in range(j) if i != e) for j in range(n + 1)] for e in range(n)]
-
-    cut = []
-    for e in range(n):
-        edges = [b for b in land[e] if b >= MINCOLS and land[e][n] - b >= MINCOLS]
-        cut.append(min(edges, key=lambda b: abs(2 * b - land[e][n])) if edges else None)
-
-    def run(kind, j, e):
-        piece = 1 if cut[e] is not None and land[e][j] >= cut[e] else 0
-        return {"kind": kind, "dst": cores[e], "buf": "b", "src_lo": off[j][e], "dst_lo": land[e][j], "w": cnt[j][e],
-                "bytes": cnt[j][e] * (1 if kind else 4), "sem": "arr%d" % piece}
+    half = off[0][n] // 2
+    world = (max(topo.host(c) for c in cores) + 1) * topo.CORES_PER_HOST
 
     def same_chip(a, b):
         return topo.host(a) == topo.host(b) and topo.chip(a) == topo.chip(b)
 
-    calls = {}
+    def is_far(j, e):
+        return not topo.may_write(cores[j], cores[e])
+
+    def in_half(j, e):
+        a, b = off[j][e], off[j][e + 1]
+        return [(h, lo, hi) for h, (lo, hi) in enumerate(((a, min(b, half)), (max(a, half), b))) if lo < hi]
+
+    first = []
+    for j in range(n):
+        w = [(0, 0), (0, 0)]
+        for e in range(n):
+            if e != j and cnt[j][e] and is_far(j, e):
+                for h, lo, hi in in_half(j, e):
+                    w[h] = (w[h][0] + 1, w[h][1] + hi - lo)
+        first.append(0 if w[0] > w[1] else 1)
+
+    def far_parts(j, e):
+        parts = in_half(j, e)
+        if len(parts) == 1 or cnt[j][e] > half:
+            return [(0 if h == first[j] else 1, lo, hi) for h, lo, hi in parts]
+        return [(1, off[j][e], off[j][e + 1])]
+
+    where, pieces = {}, []
+    for e in range(n):
+        groups = [[], [], []]
+        for j in range(n):
+            if j == e or not cnt[j][e]:
+                continue
+            if not is_far(j, e):
+                groups[0].append((j, off[j][e], off[j][e + 1]))
+            else:
+                for s, lo, hi in far_parts(j, e):
+                    groups[1 + s].append((j, lo, hi))
+        merged, cur = [], []
+        for grp in groups:
+            if not grp:
+                continue
+            cur = cur + grp
+            if merged or sum(p[2] - p[1] for p in cur) >= MINCOLS:
+                merged.append(sorted(cur))
+                cur = []
+        if cur:
+            merged[-1] = sorted(merged[-1] + cur)
+        made = []
+        for parts in merged:
+            width = sum(p[2] - p[1] for p in parts)
+            edges = [(sum(p[2] - p[1] for p in parts[:i]), i) for i in range(1, len(parts))]
+            edges = [x for x in edges if x[0] >= MINCOLS and width - x[0] >= MINCOLS]
+            if width > 2 * MINCOLS and edges:
+                i = min(edges, key=lambda x: abs(2 * x[0] - width))[1]
+                made += [parts[:i], parts[i:]]
+            else:
+                made.append(parts)
+        pos, out = 0, []
+        for k, parts in enumerate(made):
+            lo, segs = pos, []
+            for j, a, b in parts:
+                ycol = sum(cnt[i][e] for i in range(j)) + a - off[j][e]
+                where[(j, e, a)] = (pos, k)
+                if segs and segs[-1][2] + segs[-1][1] - segs[-1][0] == ycol:
+                    segs[-1] = (segs[-1][0], pos + b - a, segs[-1][2])
+                else:
+                    segs.append((pos, pos + b - a, ycol))
+                pos += b - a
+            out.append({"lo": lo, "hi": pos, "segs": segs})
+        pieces.append(out)
+
+    def run(kind, j, e, a, b):
+        pos, k = where[(j, e, a)]
+        return {"kind": kind, "dst": cores[e], "buf": "b", "src_lo": a, "dst_lo": pos, "w": b - a,
+                "bytes": (b - a) * (1 if kind else 4), "sem": "arr%d" % k}
+
+    def work(j, e, a):
+        p = pieces[e][where[(j, e, a)][1]]
+        return p["hi"] - p["lo"]
+
+    calls, stage_calls, prog, used = {}, {}, {}, set(cores)
+    todo, stretch, away = {}, {}, {}
+    for j in range(n):
+        todo[j] = sorted([e for e in range(n) if e != j and cnt[j][e]], key=lambda e: -tot[e])
+        for s in (0, 1):
+            stretch[(j, s)] = [(e, lo, hi) for e in todo[j] if is_far(j, e) for ss, lo, hi in far_parts(j, e) if ss == s]
+            stretch[(j, s)].sort(key=lambda p: -work(j, p[0], p[1]))
+        straight = [e for e in todo[j] if not is_far(j, e) and not same_chip(cores[j], cores[e])]
+        away[j] = None
+        if len(straight) <= 1 and stretch[(j, 0)] and stretch[(j, 1)]:
+            one = [s for s in (0, 1) if all(same_chip(cores[p[0]], cores[stretch[(j, s)][0][0]]) for p in stretch[(j, s)])]
+            away[j] = one[0] if one else None
+
+    pairs = {}
+
+    def widest(j):
+        return max(p[2] - p[1] for p in stretch[(j, away[j])]) if away[j] is not None else 0
+
+    for j in sorted(range(n), key=lambda j: -widest(j)):
+        c = cores[j]
+        able = [k for k in range(world) if k not in used and topo.die(k) == topo.die(c) and topo.may_write(c, k)
+                and all(topo.may_write(k, d) for d in cores)]
+        home = [k for k in able if same_chip(k, c)][:2]
+        used.update(home)
+        pairs[(j, 0)] = pairs[(j, 1)] = home
+        if away[j] is not None:
+            there = [k for k in able if topo.mates(k, cores[stretch[(j, away[j])][0][0]])][:2]
+            pairs[(j, away[j])] = there
+            used.update(there)
+
     for j, c in enumerate(cores):
-        todo = sorted([e for e in range(n) if e != j and cnt[j][e]], key=lambda e: -tot[e])
-        far = [e for e in todo if not topo.may_write(c, cores[e])]
-        near = [e for e in todo if topo.may_write(c, cores[e])]
-        mine = []
-        if far:
-            chipmates = [k for k in range(max(0, c - topo.CORES_PER_CHIP), c + topo.CORES_PER_CHIP)
-                         if same_chip(k, c) and k not in cores]
-            helpers = [k for k in chipmates if topo.die(k) == topo.die(c) and all(topo.may_write(k, d) for d in cores)]
-            lo, hi = min(off[j][e] for e in far), max(off[j][e + 1] for e in far)
+        stage_calls[c] = [[], []]
+        for s in (0, 1):
+            parts = stretch[(j, s)]
+            if not parts:
+                continue
+            lo, hi = min(p[1] for p in parts), max(p[2] for p in parts)
             for kind in (0, 1):
-                mine.append([{"kind": kind, "dst": helpers[kind], "buf": "x", "src_lo": lo, "dst_lo": lo, "w": hi - lo,
-                              "bytes": (hi - lo) * (1 if kind else 4), "sem": "hop"}])
-                calls[helpers[kind]] = _pair_up([run(kind, j, e) for e in far], True)
-        calls[c] = mine + _pair_up([run(kind, j, e) for e in near for kind in (0, 1)], False)
+                helper = pairs[(j, s)][kind]
+                stage_calls[c][s].append([{"kind": kind, "dst": helper, "buf": "x", "src_lo": lo, "dst_lo": lo,
+                                           "w": hi - lo, "bytes": (hi - lo) * (1 if kind else 4), "sem": "hop%d" % s}])
+                cl = _pair_up([run(kind, j, e, a, b) for e, a, b in parts], True)
+                prog.setdefault(helper, []).append(("hop%d" % s, cl))
+                calls[helper] = calls.get(helper, []) + cl
+        near = sorted([e for e in todo[j] if not is_far(j, e)], key=lambda e: -work(j, e, off[j][e]))
+        stage_calls[c][1] += _pair_up([run(kind, j, e, off[j][e], off[j][e + 1]) for e in near for kind in (0, 1)], False)
+        calls[c] = stage_calls[c][0] + stage_calls[c][1]
 
     need, sent = {}, {}
     for c, cl in calls.items():
@@ -98,15 +197,18 @@ def _plan(T, topo):
             for t in call:
                 m = topo.mask(c, t["dst"])
                 t["mask"] = (m & ~leaving) or m if same_chip(c, t["dst"]) else m
+                if t["sem"] == "hop0" and t["kind"] == 1 and same_chip(c, t["dst"]) and (m & leaving):
+                    t["mask"] = m & leaving
             if len(call) > 1 and call[0]["mask"] & call[1]["mask"]:
-                half = min(len(_bits(t["mask"])) for t in call) // 2
+                k2 = min(len(_bits(t["mask"])) for t in call) // 2
                 for i, t in enumerate(call):
-                    t["mask"] = _pick(t["mask"], i * half, half)
+                    t["mask"] = _pick(t["mask"], i * k2, k2)
             for t in call:
                 k = len(_bits(t["mask"]))
                 need[(t["dst"], t["sem"])] = need.get((t["dst"], t["sem"]), 0) + k
                 sent[c] = sent.get(c, 0) + k
-    return {"off": off, "tot": tot, "land": land, "cut": cut, "calls": calls, "need": need, "sent": sent, "cnt": cnt}
+    return {"off": off, "calls": calls, "stage": stage_calls, "need": need, "sent": sent, "cnt": cnt, "first": first,
+            "pieces": pieces, "half": half, "prog": prog}
 
 
 def _issue(g, T, topo, core, call):
@@ -137,71 +239,82 @@ def rank_program(g, core, T, topo):
     P = _MEMO["plan"]
     S = T.sem
     rank = T.rank_of(core)
-    calls = P["calls"].get(core, [])
 
     if rank is None:
-        if not calls:
+        if core not in P["prog"]:
             return
-        g.wait_ge(S.hop, P["need"][(core, "hop")])
-        for call in calls:
-            _issue(g, T, topo, core, call)
+        for sem, calls in P["prog"][core]:
+            g.wait_ge(S[sem], P["need"][(core, sem)])
+            for call in calls:
+                _issue(g, T, topo, core, call)
         g.wait_ge(S.sent, P["sent"][core])
         return
 
-    e, cnt, off, land, n = rank, P["cnt"], P["off"], P["land"], len(P["cnt"])
+    e, cnt, off, half = rank, P["cnt"], P["off"], P["half"]
     own = cnt[e][e]
     ncols = T.xq.shape[1]
+    h0 = P["first"][e]
+    cols = [(h * half, h * half + half) for h in (h0, 1 - h0)]
 
-    g.sync.dma_start(T.xb[:], T.x[:]).then_inc(S.ldx, 16)
+    for s, queue in enumerate((g.sync, g.scalar)):
+        a, b = cols[s]
+        queue.dma_start(T.xb[:, 4 * a:4 * b], T.x[:, 4 * a:4 * b]).then_inc(S["ld%d" % s], 16)
     g.sync.dma_start(T.wb[:], T.w[:]).then_inc(S.ldw, 16)
-    g.vector.wait_ge(S.ldx, 16)
-    g.vector.quantize_mx(T.xq[:], T.xs[:], T.xb[:]).then_inc(S.qx, 1)
+    for s in (0, 1):
+        a, b = cols[s]
+        g.vector.wait_ge(S["ld%d" % s], 16)
+        g.vector.quantize_mx(T.xq[:, a:b], T.xs[:, a:b], T.xb[:, 4 * a:4 * b]).then_inc(S["q%d" % s], 1)
     g.vector.wait_ge(S.ldw, 16)
     g.vector.quantize_mx(T.wq[:], T.ws[:], T.wb[:]).then_inc(S.qw, 1)
 
-    g.wait_ge(S.qx, 1)
-    for call in calls:
-        _issue(g, T, topo, core, call)
+    for s in (0, 1):
+        g.wait_ge(S["q%d" % s], 1)
+        for call in P["stage"][core][s]:
+            _issue(g, T, topo, core, call)
 
-    total, c = land[e][n], P["cut"][e]
-    pieces = [(0, total, 0)] if c is None else [(0, c, 0), (c, total, 1)]
+    nst = {"sts": 0, "stc": 0}
 
-    def widest(p):
-        return max(cnt[j][e] for j in range(n) if j != e and p[0] <= land[e][j] < p[1])
-    pieces.sort(key=widest)
-    own_at = land[e][e]
+    def store(k, y0, y1):
+        queue, sem = ((g.sync, "sts"), (g.scalar, "stc"))[k % 2]
+        queue.dma_start(T.y[:, y0:y1], T.ysb[:, y0:y1]).then_inc(S[sem], 16)
+        nst[sem] += 16
 
     g.tensor.wait_ge(S.qw, 1)
     if own:
         a = min(off[e][e], ncols - MINCOLS)
-        g.tensor.wait_ge(S.qx, 1)
-        g.tensor.matmul_mx(T.ps[:, 2 * BANK:2 * BANK + MINCOLS], T.wq[:], T.ws[:], T.xq[:, a:a + MINCOLS],
+        y0 = sum(cnt[i][e] for i in range(e))
+        g.tensor.wait_ge(S.q0, 1)
+        g.tensor.wait_ge(S.q1, 1)
+        g.tensor.matmul_mx(T.ps[:, 4 * BANK:4 * BANK + MINCOLS], T.wq[:], T.ws[:], T.xq[:, a:a + MINCOLS],
                            T.xs[:, a:a + MINCOLS], True, True).then_inc(S.mmo, 1)
-        home = [k for k, p in enumerate(pieces) if p[0] <= own_at <= p[1]][0]
         g.vector.wait_ge(S.mmo, 1)
-        g.vector.tensor_copy(T.ysb[:, own_at:own_at + own],
-                             T.ps[:, 2 * BANK + off[e][e] - a:2 * BANK + off[e][e] - a + own]).then_inc(S["cp%d" % home], 1)
+        g.vector.tensor_copy(T.ysb[:, y0:y0 + own],
+                             T.ps[:, 4 * BANK + off[e][e] - a:4 * BANK + off[e][e] - a + own]).then_inc(S.cpo, 1)
+        g.sync.wait_ge(S.cpo, 1)
+        store(0, y0, y0 + own)
 
-    for k, (lo, hi, piece) in enumerate(pieces):
-        g.tensor.wait_ge(S["arr%d" % piece], P["need"][(core, "arr%d" % piece)])
+    pieces = P["pieces"][e]
+    for k, p in enumerate(pieces):
+        lo, hi = min(p["lo"], p["hi"] - MINCOLS), p["hi"]
+        g.tensor.wait_ge(S["arr%d" % k], P["need"][(core, "arr%d" % k)])
         g.tensor.matmul_mx(T.ps[:, k * BANK:k * BANK + hi - lo], T.wq[:], T.ws[:], T.bq[:, lo:hi], T.bs[:, lo:hi],
                            True, True).then_inc(S["mm%d" % k], 1)
-        segs = [(lo, hi, 0)] if not own else [s for s in ((lo, min(hi, own_at), 0), (max(lo, own_at), hi, own)) if s[0] < s[1]]
-        eng, queue = (g.vector, g.sync) if k == 0 else (g.scalar, g.scalar)
+        on_vector = (len(pieces) - 1 - k) % 2 == 0
+        eng = g.vector if on_vector else g.scalar
         eng.wait_ge(S["mm%d" % k], 1)
-        done = 0
-        for a, b, shift in segs:
-            src, dst = T.ps[:, k * BANK + a - lo:k * BANK + b - lo], T.ysb[:, a + shift:b + shift]
-            if k == 0:
+        for a, b, y0 in p["segs"]:
+            src, dst = T.ps[:, k * BANK + a - lo:k * BANK + b - lo], T.ysb[:, y0:y0 + b - a]
+            if on_vector:
                 eng.tensor_copy(dst, src).then_inc(S["cp%d" % k], 1)
             else:
                 eng.activation(dst, src, ActivationFunctionType.Copy).then_inc(S["cp%d" % k], 1)
-            done += 1
-        y0, y1 = min(s[0] + s[2] for s in segs), max(s[1] + s[2] for s in segs)
-        if own and home == k:
-            y0, y1, done = min(y0, own_at), max(y1, own_at + own), done + 1
-        queue.wait_ge(S["cp%d" % k], done)
-        queue.dma_start(T.y[:, y0:y1], T.ysb[:, y0:y1]).then_inc(S["st%d" % k], 16)
-        queue.wait_ge(S["st%d" % k], 16)
+        queues = (g.sync, g.scalar)[:len(p["segs"])]
+        for queue in queues:
+            queue.wait_ge(S["cp%d" % k], len(p["segs"]))
+        for i, (a, b, y0) in enumerate(p["segs"]):
+            store(i, y0, y0 + b - a)
 
+    g.sync.wait_ge(S.sts, nst["sts"])
+    if nst["stc"]:
+        g.scalar.wait_ge(S.stc, nst["stc"])
     g.wait_ge(S.sent, P["sent"][core])

from concourse.bass import DstId, RemoteDMATransfer
from concourse.mybir import dt, ActivationFunctionType

MINCOLS = 128
BANK = 512

SCRATCH = {
    "xb": ("sbuf", [128, 1024], "bfloat16"),
    "wb": ("sbuf", [128, 512], "bfloat16"),
    "xq": ("sbuf", [128, 256], "float8_e4m3fn_x4"),
    "xs": ("sbuf", [128, 256], "uint8"),
    "wq": ("sbuf", [128, 128], "float8_e4m3fn_x4"),
    "ws": ("sbuf", [128, 128], "uint8"),
    "bq": ("sbuf", [128, 464], "float8_e4m3fn_x4"),
    "bs": ("sbuf", [128, 464], "uint8"),
    "ysb": ("sbuf", [128, 464], "float32"),
    "ps": ("psum", [128, 5 * BANK], "float32"),
}
SEMAPHORES = ["ld0", "ld1", "ldw", "q0", "q1", "qw", "hop0", "hop1", "arr0", "arr1", "arr2", "arr3", "sent", "mmo", "mm0",
              "mm1", "mm2", "mm3", "cpo", "cp0", "cp1", "cp2", "cp3", "sts", "stc"]

_MEMO = {}


def _bits(mask):
    return [b for b in range(mask.bit_length()) if (mask >> b) & 1]


def _pick(mask, start, n):
    m = 0
    for b in _bits(mask)[start:start + n]:
        m |= 1 << b
    return m


def _pair_up(items, first_alone):
    calls, rest = [], list(items)
    while rest:
        a = rest.pop(0)
        mate = None
        if not (first_alone and not calls):
            for b in rest:
                if b["bytes"] == a["bytes"]:
                    mate = b
                    break
        if mate is None:
            calls.append([a])
        else:
            rest.remove(mate)
            calls.append([a, mate])
    return calls


def _plan(T, topo):
    cores, cnt = list(T.cores), T.tables["CNT"]
    n = len(cores)
    off = [[sum(r[:e]) for e in range(n + 1)] for r in cnt]
    tot = [sum(cnt[j][e] for j in range(n)) for e in range(n)]
    half = off[0][n] // 2
    world = (max(topo.host(c) for c in cores) + 1) * topo.CORES_PER_HOST

    def same_chip(a, b):
        return topo.host(a) == topo.host(b) and topo.chip(a) == topo.chip(b)

    def is_far(j, e):
        return not topo.may_write(cores[j], cores[e])

    def in_half(j, e):
        a, b = off[j][e], off[j][e + 1]
        return [(h, lo, hi) for h, (lo, hi) in enumerate(((a, min(b, half)), (max(a, half), b))) if lo < hi]

    first = []
    for j in range(n):
        w = [(0, 0), (0, 0)]
        for e in range(n):
            if e != j and cnt[j][e] and is_far(j, e):
                for h, lo, hi in in_half(j, e):
                    w[h] = (w[h][0] + 1, w[h][1] + hi - lo)
        first.append(0 if w[0] > w[1] else 1)

    def far_parts(j, e):
        parts = in_half(j, e)
        if len(parts) == 1 or cnt[j][e] > half:
            return [(0 if h == first[j] else 1, lo, hi) for h, lo, hi in parts]
        return [(1, off[j][e], off[j][e + 1])]

    where, pieces = {}, []
    for e in range(n):
        groups = [[], [], []]
        for j in range(n):
            if j == e or not cnt[j][e]:
                continue
            if not is_far(j, e):
                groups[0].append((j, off[j][e], off[j][e + 1]))
            else:
                for s, lo, hi in far_parts(j, e):
                    groups[1 + s].append((j, lo, hi))
        merged, cur = [], []
        for grp in groups:
            if not grp:
                continue
            cur = cur + grp
            if merged or sum(p[2] - p[1] for p in cur) >= MINCOLS:
                merged.append(sorted(cur))
                cur = []
        if cur:
            merged[-1] = sorted(merged[-1] + cur)
        made = []
        for parts in merged:
            width = sum(p[2] - p[1] for p in parts)
            edges = [(sum(p[2] - p[1] for p in parts[:i]), i) for i in range(1, len(parts))]
            edges = [x for x in edges if x[0] >= MINCOLS and width - x[0] >= MINCOLS]
            if width > 2 * MINCOLS and edges:
                i = min(edges, key=lambda x: abs(2 * x[0] - width))[1]
                made += [parts[:i], parts[i:]]
            else:
                made.append(parts)
        pos, out = 0, []
        for k, parts in enumerate(made):
            lo, segs = pos, []
            for j, a, b in parts:
                ycol = sum(cnt[i][e] for i in range(j)) + a - off[j][e]
                where[(j, e, a)] = (pos, k)
                if segs and segs[-1][2] + segs[-1][1] - segs[-1][0] == ycol:
                    segs[-1] = (segs[-1][0], pos + b - a, segs[-1][2])
                else:
                    segs.append((pos, pos + b - a, ycol))
                pos += b - a
            out.append({"lo": lo, "hi": pos, "segs": segs})
        pieces.append(out)

    def run(kind, j, e, a, b):
        pos, k = where[(j, e, a)]
        return {"kind": kind, "dst": cores[e], "buf": "b", "src_lo": a, "dst_lo": pos, "w": b - a,
                "bytes": (b - a) * (1 if kind else 4), "sem": "arr%d" % k}

    def work(j, e, a):
        p = pieces[e][where[(j, e, a)][1]]
        return p["hi"] - p["lo"]

    calls, stage_calls, prog, used = {}, {}, {}, set(cores)
    todo, stretch, away = {}, {}, {}
    for j in range(n):
        todo[j] = sorted([e for e in range(n) if e != j and cnt[j][e]], key=lambda e: -tot[e])
        for s in (0, 1):
            stretch[(j, s)] = [(e, lo, hi) for e in todo[j] if is_far(j, e) for ss, lo, hi in far_parts(j, e) if ss == s]
            stretch[(j, s)].sort(key=lambda p: -work(j, p[0], p[1]))
        straight = [e for e in todo[j] if not is_far(j, e) and not same_chip(cores[j], cores[e])]
        away[j] = None
        if len(straight) <= 1 and stretch[(j, 0)] and stretch[(j, 1)]:
            one = [s for s in (0, 1) if all(same_chip(cores[p[0]], cores[stretch[(j, s)][0][0]]) for p in stretch[(j, s)])]
            away[j] = one[0] if one else None

    pairs = {}

    def widest(j):
        return max(p[2] - p[1] for p in stretch[(j, away[j])]) if away[j] is not None else 0

    for j in sorted(range(n), key=lambda j: -widest(j)):
        c = cores[j]
        able = [k for k in range(world) if k not in used and topo.die(k) == topo.die(c) and topo.may_write(c, k)
                and all(topo.may_write(k, d) for d in cores)]
        home = [k for k in able if same_chip(k, c)][:2]
        used.update(home)
        pairs[(j, 0)] = pairs[(j, 1)] = home
        if away[j] is not None:
            there = [k for k in able if topo.mates(k, cores[stretch[(j, away[j])][0][0]])][:2]
            pairs[(j, away[j])] = there
            used.update(there)

    for j, c in enumerate(cores):
        stage_calls[c] = [[], []]
        for s in (0, 1):
            parts = stretch[(j, s)]
            if not parts:
                continue
            lo, hi = min(p[1] for p in parts), max(p[2] for p in parts)
            for kind in (0, 1):
                helper = pairs[(j, s)][kind]
                stage_calls[c][s].append([{"kind": kind, "dst": helper, "buf": "x", "src_lo": lo, "dst_lo": lo,
                                           "w": hi - lo, "bytes": (hi - lo) * (1 if kind else 4), "sem": "hop%d" % s}])
                cl = _pair_up([run(kind, j, e, a, b) for e, a, b in parts], True)
                prog.setdefault(helper, []).append(("hop%d" % s, cl))
                calls[helper] = calls.get(helper, []) + cl
        near = sorted([e for e in todo[j] if not is_far(j, e)], key=lambda e: -work(j, e, off[j][e]))
        stage_calls[c][1] += _pair_up([run(kind, j, e, off[j][e], off[j][e + 1]) for e in near for kind in (0, 1)], False)
        calls[c] = stage_calls[c][0] + stage_calls[c][1]

    need, sent = {}, {}
    for c, cl in calls.items():
        leaving = 0
        for call in cl:
            for t in call:
                if not same_chip(c, t["dst"]):
                    leaving |= topo.mask(c, t["dst"])
        for call in cl:
            for t in call:
                m = topo.mask(c, t["dst"])
                t["mask"] = (m & ~leaving) or m if same_chip(c, t["dst"]) else m
                if t["sem"] == "hop0" and t["kind"] == 1 and same_chip(c, t["dst"]) and (m & leaving):
                    t["mask"] = m & leaving
            if len(call) > 1 and call[0]["mask"] & call[1]["mask"]:
                k2 = min(len(_bits(t["mask"])) for t in call) // 2
                for i, t in enumerate(call):
                    t["mask"] = _pick(t["mask"], i * k2, k2)
            for t in call:
                k = len(_bits(t["mask"]))
                need[(t["dst"], t["sem"])] = need.get((t["dst"], t["sem"]), 0) + k
                sent[c] = sent.get(c, 0) + k
    return {"off": off, "calls": calls, "stage": stage_calls, "need": need, "sent": sent, "cnt": cnt, "first": first,
            "pieces": pieces, "half": half, "prog": prog}


def _issue(g, T, topo, core, call):
    trs = []
    for t in call:
        a, b, w = t["src_lo"], t["dst_lo"], t["w"]
        if t["kind"] == 0:
            src = T.xq[:, a:a + w].bitcast(dt.uint8)
            dst = (T.xq if t["buf"] == "x" else T.bq)[:, b:b + w].bitcast(dt.uint8)
        else:
            src = T.xs[:, a:a + w]
            dst = (T.xs if t["buf"] == "x" else T.bs)[:, b:b + w]
        rid, pid = topo.addr(t["dst"], core)
        trs.append((dst, src, T.sem[t["sem"]], pid, rid, t["mask"]))
    if len(trs) == 1:
        dst, src, sem, pid, rid, mask = trs[0]
        g.remote_dma(out_ap=dst, in_ap=src, remote_sem=sem, local_sem=T.sem.sent, pid=pid, routing_id=rid,
                     dma_engine_mask=mask)
    else:
        g.remote_dma_fused([RemoteDMATransfer(dst_ids=[DstId(rid=rid, pnc=pid)], dma_engine_mask=mask, remote_sem=sem,
                                              src=src, dst=dst) for dst, src, sem, pid, rid, mask in trs],
                           local_sem=T.sem.sent)


def rank_program(g, core, T, topo):
    if "plan" not in _MEMO:
        _MEMO["plan"] = _plan(T, topo)
    P = _MEMO["plan"]
    S = T.sem
    rank = T.rank_of(core)

    if rank is None:
        if core not in P["prog"]:
            return
        for sem, calls in P["prog"][core]:
            g.wait_ge(S[sem], P["need"][(core, sem)])
            for call in calls:
                _issue(g, T, topo, core, call)
        g.wait_ge(S.sent, P["sent"][core])
        return

    e, cnt, off, half = rank, P["cnt"], P["off"], P["half"]
    own = cnt[e][e]
    ncols = T.xq.shape[1]
    h0 = P["first"][e]
    cols = [(h * half, h * half + half) for h in (h0, 1 - h0)]

    for s, queue in enumerate((g.sync, g.scalar)):
        a, b = cols[s]
        queue.dma_start(T.xb[:, 4 * a:4 * b], T.x[:, 4 * a:4 * b]).then_inc(S["ld%d" % s], 16)
    g.sync.dma_start(T.wb[:], T.w[:]).then_inc(S.ldw, 16)
    for s in (0, 1):
        a, b = cols[s]
        g.vector.wait_ge(S["ld%d" % s], 16)
        g.vector.quantize_mx(T.xq[:, a:b], T.xs[:, a:b], T.xb[:, 4 * a:4 * b]).then_inc(S["q%d" % s], 1)
    g.vector.wait_ge(S.ldw, 16)
    g.vector.quantize_mx(T.wq[:], T.ws[:], T.wb[:]).then_inc(S.qw, 1)

    for s in (0, 1):
        g.wait_ge(S["q%d" % s], 1)
        for call in P["stage"][core][s]:
            _issue(g, T, topo, core, call)

    nst = {"sts": 0, "stc": 0}

    def store(k, y0, y1):
        queue, sem = ((g.sync, "sts"), (g.scalar, "stc"))[k % 2]
        queue.dma_start(T.y[:, y0:y1], T.ysb[:, y0:y1]).then_inc(S[sem], 16)
        nst[sem] += 16

    g.tensor.wait_ge(S.qw, 1)
    if own:
        a = min(off[e][e], ncols - MINCOLS)
        y0 = sum(cnt[i][e] for i in range(e))
        g.tensor.wait_ge(S.q0, 1)
        g.tensor.wait_ge(S.q1, 1)
        g.tensor.matmul_mx(T.ps[:, 4 * BANK:4 * BANK + MINCOLS], T.wq[:], T.ws[:], T.xq[:, a:a + MINCOLS],
                           T.xs[:, a:a + MINCOLS], True, True).then_inc(S.mmo, 1)
        g.vector.wait_ge(S.mmo, 1)
        g.vector.tensor_copy(T.ysb[:, y0:y0 + own],
                             T.ps[:, 4 * BANK + off[e][e] - a:4 * BANK + off[e][e] - a + own]).then_inc(S.cpo, 1)
        g.sync.wait_ge(S.cpo, 1)
        store(0, y0, y0 + own)

    pieces = P["pieces"][e]
    for k, p in enumerate(pieces):
        lo, hi = min(p["lo"], p["hi"] - MINCOLS), p["hi"]
        g.tensor.wait_ge(S["arr%d" % k], P["need"][(core, "arr%d" % k)])
        g.tensor.matmul_mx(T.ps[:, k * BANK:k * BANK + hi - lo], T.wq[:], T.ws[:], T.bq[:, lo:hi], T.bs[:, lo:hi],
                           True, True).then_inc(S["mm%d" % k], 1)
        on_vector = (len(pieces) - 1 - k) % 2 == 0
        eng = g.vector if on_vector else g.scalar
        eng.wait_ge(S["mm%d" % k], 1)
        for a, b, y0 in p["segs"]:
            src, dst = T.ps[:, k * BANK + a - lo:k * BANK + b - lo], T.ysb[:, y0:y0 + b - a]
            if on_vector:
                eng.tensor_copy(dst, src).then_inc(S["cp%d" % k], 1)
            else:
                eng.activation(dst, src, ActivationFunctionType.Copy).then_inc(S["cp%d" % k], 1)
        queues = (g.sync, g.scalar)[:len(p["segs"])]
        for queue in queues:
            queue.wait_ge(S["cp%d" % k], len(p["segs"]))
        for i, (a, b, y0) in enumerate(p["segs"]):
            store(i, y0, y0 + b - a)

    g.sync.wait_ge(S.sts, nst["sts"])
    if nst["stc"]:
        g.scalar.wait_ge(S.stc, nst["stc"])
    g.wait_ge(S.sent, P["sent"][core])
